import numpy as np
import ml_dtypes


def mxq(x, axis, fmt="e4m3"):
    dtype, down = {"e4m3": (ml_dtypes.float8_e4m3fn, 7), "e5m2": (ml_dtypes.float8_e5m2, 14)}[fmt]
    v = np.moveaxis(np.asarray(x, np.float32).astype(ml_dtypes.bfloat16).astype(np.float64), axis, -1)
    blocks = v.reshape(v.shape[:-1] + (-1, 32))
    amax = np.abs(blocks).max(-1, keepdims=True)
    byte = np.maximum(np.where(amax > 0, np.frexp(amax)[1] - 1 + 127, 0) - down, 1)
    scale = np.exp2(byte - 127.0)
    codes = (blocks / scale).astype(np.float32).astype(dtype).astype(np.float64)
    return np.moveaxis((codes * scale).reshape(v.shape), -1, axis)


WIDE = False


def mx_kscale(k):
    if not WIDE:
        return np.ones(k)
    levels = np.array([10, -10, 5, -5, 0])
    if k % 512:
        return np.exp2(np.random.permutation(np.resize(levels, k // 32))).repeat(32)
    a = np.empty((k // 512, 16))
    for p in range(k // 512):
        a[p, :8] = np.random.permutation(np.resize(levels, 8))
        for g in range(8):
            far = levels[np.abs(levels - a[p, g]) >= 10]
            a[p, g + 8] = far[np.random.randint(len(far))]
    return np.exp2(a.ravel()).repeat(32)


def f64(x):
    return np.asarray(x).astype(np.float64)


def striped(idx):
    return np.tile(idx.reshape(-1, 16).T, (8, 1)).astype(np.uint16)


def unstriped(offs):
    return offs[:16].T.reshape(-1).astype(np.int64)


E2M1 = np.array([0.0, 0.5, 1.0, 1.5, 2.0, 3.0, 4.0, 6.0, -0.0, -0.5, -1.0, -1.5, -2.0, -3.0, -4.0, -6.0])


def pack_weight(w, fmt):
    k, n = w.shape
    w = f64(np.asarray(w, np.float32).astype(ml_dtypes.bfloat16)).reshape(k // 32, 32, n)
    amax = np.abs(w).max(1)
    if fmt == "e4m3":
        byte = np.frexp(amax)[1] - 1 + 127 - 7
    else:
        mant, ex = np.frexp(amax / 6.0)
        byte = np.where(mant > 0.5, ex, ex - 1) + 127
    byte = np.clip(np.where(amax > 0, byte, 1), 1, 254)
    scaled = (w * np.exp2(127.0 - byte)[:, None, :]).reshape(k, n).astype(np.float32)
    by_word = np.ascontiguousarray(scaled.reshape(k // 512, 128, 4, n).transpose(0, 1, 3, 2))
    if fmt == "e4m3":
        words = by_word.astype(ml_dtypes.float8_e4m3fn).view(np.uint8)
    else:
        c = by_word.astype(ml_dtypes.float4_e2m1fn).view(np.uint8) & 0xF
        words = (c[..., 0::2] | (c[..., 1::2] << 4)).reshape(k // 512, 128, 2 * n)
    return np.ascontiguousarray(words), np.ascontiguousarray(byte.astype(np.uint8).reshape(k // 512, 16, n))


def unpack_weight(words, scales, fmt):
    g, _, n = scales.shape
    words = np.ascontiguousarray(words).reshape(g, 128, n, -1)
    if fmt == "e4m3":
        vals = words.view(ml_dtypes.float8_e4m3fn).astype(np.float64)
    else:
        nib = np.empty((g, 128, n, 4), np.uint8)
        nib[..., 0::2] = words & 0xF
        nib[..., 1::2] = words >> 4
        vals = E2M1[nib]
    vals = vals * np.repeat(np.exp2(scales.astype(np.float64) - 127.0), 8, axis=1)[..., None]
    return vals.transpose(0, 1, 3, 2).reshape(g * 512, n)


def gelu(v):
    return 0.5 * v * (1.0 + np.tanh(np.sqrt(2.0 / np.pi) * (v + 0.044715 * v**3)))


K, T, S, H, T2, S2, T3, P = 1024, 2048, 512, 512, 1024, 1024, 2048, 512

def setup_inputs():
    n = np.random.standard_normal
    s = mx_kscale(K)[:, None]
    u = mx_kscale(H)[:, None]
    tab_words, tab_scales = pack_weight(n((K, T)) * s, "e4m3")
    tab2_words, tab2_scales = pack_weight(n((H, T3)) / np.sqrt(H) / u, "e4m3")
    w3_words, w3_scales = pack_weight(1.5 * n((K, H)) / np.sqrt(K) / s * u.T, "e2m1")
    return {
        "tab_words": tab_words, "tab_scales": tab_scales,
        "offs": striped(np.random.permutation(T)[:S]),
        "tab2_words": tab2_words, "tab2_scales": tab2_scales,
        "offs2": striped(np.random.permutation(T3)[:S2]),
        "offs3": striped(np.random.permutation(T2)[:S]),
        "pos1": striped(np.random.permutation(T2)[:P]),
        "pos2": striped(np.random.permutation(T2)[:P]),
        "w1": (1.2 * n((K, H)) / np.sqrt(K) / s).astype(np.float32),
        "w2": (0.58 * n((K, H)) / np.sqrt(K) / s).astype(np.float32),
        "w3_words": w3_words, "w3_scales": w3_scales,
        "w4": (0.8 * n((K, S2)) / np.sqrt(K) / s).astype(np.float32),
        "wgs": np.exp(0.3 * n((128, S))).astype(np.float32),
        "page0": (0.7 * n((H, T2)) * u).astype(np.float32),
        "orbit": (0.5 * n(S2)).astype(np.float32),
    }

def reference(tab_words, tab_scales, offs, tab2_words, tab2_scales, offs2, offs3, pos1, pos2,
              w1, w2, w3_words, w3_scales, w4, wgs, page0, orbit):
    v = unpack_weight(tab_words, tab_scales, "e4m3")[:, unstriped(offs)]
    v2 = unpack_weight(tab2_words, tab2_scales, "e4m3")[:, unstriped(offs2)]
    p1 = mxq(f64(w1), 0, "e4m3").T @ v
    p2 = mxq(f64(w2), 0, "e4m3").T @ v
    p3 = unpack_weight(w3_words, w3_scales, "e2m1").T @ v
    h = (np.tanh(p1) - np.sin(p2)) * p3
    page = f64(page0).copy()
    page[:, unstriped(offs3)] = np.tile(f64(wgs), (H // 128, 1)) * h
    e = v2.T @ mxq(page, 0, "e4m3")
    f = mxq(f64(w4), 0, "e4m3").T @ v
    d = e[:, unstriped(pos1)] - e[:, unstriped(pos2)]
    return np.maximum(d, f) + f64(orbit)[:, None]

@@ -1,0 +1,292 @@
+import math
+from contextlib import ExitStack
+
+import concourse.mybir as mybir
+from concourse.masks import make_identity
+
+K, T, S, H, T2, S2, T3, PAIRS = 1024, 2048, 512, 512, 1024, 1024, 2048, 512
+FLOPS = 2 * (3 * K * H * S + H * S2 * T2 + K * S2 * S)
+
+F32 = mybir.dt.float32
+BF16 = mybir.dt.bfloat16
+I32 = mybir.dt.int32
+U32 = mybir.dt.uint32
+U16 = mybir.dt.uint16
+U8 = mybir.dt.uint8
+FP8X4 = mybir.dt.float8_e4m3fn_x4
+FP4X4 = mybir.dt.float4_e2m1fn_x4
+ALU = mybir.AluOpType
+ACT = mybir.ActivationFunctionType
+
+P = 128
+PACK = 4
+K_PASS = P * PACK
+PASSES = K // K_PASS
+CHUNK = 256
+BANK = 512
+QUADS = 4
+TURN = 2.0 * math.pi
+
+
+def tile_list_tracklet_orbit_features_kernel(
+    tc, tab_words, tab_scales, offs, tab2_words, tab2_scales, offs2, offs3, pos1, pos2,
+    w1, w2, w3_words, w3_scales, w4, wgs, page0, orbit, out,
+):
+    nc = tc.nc
+    with ExitStack() as ctx:
+        keep = ctx.enter_context(tc.tile_pool(name="keep", bufs=1))
+        ring3 = ctx.enter_context(tc.tile_pool(name="ring3", bufs=3))
+        ring2 = ctx.enter_context(tc.tile_pool(name="ring2", bufs=2))
+        psum = ctx.enter_context(tc.psum_pool(name="psum", bufs=1))
+
+        def bank(b, shape):
+            return psum.tile(shape, F32, name="bank%d" % b, tag="bank%d" % b)
+
+        def load_list(name, src):
+            tile = keep.tile(list(src.shape), U16, name=name)
+            nc.sync.dma_start(tile[:], src)
+            return tile
+
+        def interleaved(tag):
+            return keep.tile([P, BANK * PACK], BF16, name=tag, tag=tag, align_bytes=64)
+
+        def cleared_plane(name, src, clearer):
+            plane = keep.tile([P, src.shape[0] * src.shape[2]], U8, name=name, align_bytes=64)
+            clearer.memset(plane[:].bitcast(I32), 0)
+            return plane
+
+        def load_scale_rows(plane, src, queue):
+            passes = src.shape[0]
+            for quad in range(QUADS):
+                queue.dma_start(
+                    plane[32 * quad : 32 * quad + 4, :].bitcast(I32).rearrange("r (a c) -> r a c", a=passes),
+                    src[:, 4 * quad : 4 * quad + 4, :].bitcast(I32).rearrange("a r c -> r a c"),
+                )
+
+        def load_words(name, src):
+            tile = keep.tile([P, src.shape[1]], U32, name=name, align_bytes=64)
+            nc.sync.dma_start(tile[:].bitcast(I32), src.rearrange("p t i -> p (t i)").bitcast(I32))
+            return tile
+
+        def load_weight(name, w, chunk, a):
+            raw = keep.tile([P, PACK, CHUNK], F32, name="raw", tag="%s_raw%d%d" % (name, chunk, a), align_bytes=64)
+            rows = w[a * K_PASS : (a + 1) * K_PASS, chunk * CHUNK : (chunk + 1) * CHUNK]
+            nc.sync.dma_start(raw[:], rows.rearrange("(p j) c -> p j c", j=PACK))
+            return raw
+
+        def quantise_weight(name, raw_passes, grouped_tag, codes_tag=None):
+            grouped = interleaved(grouped_tag)
+            cast_weight(raw_passes, grouped)
+            return quantise(name, grouped, codes_tag or name)
+
+        def cast_weight(raw_passes, grouped):
+            for a in range(PASSES):
+                dst = grouped[:, a * CHUNK * PACK : (a + 1) * CHUNK * PACK]
+                dst = dst.rearrange("p (c i t) -> p c t i", i=4, t=PACK)
+                src = raw_passes[a][:].rearrange("p t (c i) -> p c t i", i=4)
+                nc.scalar.copy(dst, src)
+
+        def quantise(name, grouped, codes_tag):
+            codes = keep.tile([P, BANK], U32, name=name + "_codes", tag=codes_tag, align_bytes=64)
+            scales = keep.tile([P, BANK], U8, name=name + "_scales", align_bytes=64)
+            nc.vector.quantize_mx(out=codes[:].bitcast(FP8X4), scales=scales[:], in_=grouped[:])
+            return codes, scales
+
+        tab_planes = cleared_plane("tab_planes", tab_scales, nc.vector)
+        warm = keep.tile([P, 2], F32, name="warm")
+        nc.vector.memset(warm[:, 0:1], 0.0)
+        nc.scalar.activation(warm[:, 1:2], warm[:, 0:1], ACT.Silu)
+        w3_planes = cleared_plane("w3_planes", w3_scales, nc.gpsimd)
+        tab2_planes = cleared_plane("tab2_planes", tab2_scales, nc.gpsimd)
+        identity = keep.tile([P, P], F32, name="identity")
+        make_identity(nc, identity[:])
+
+        def load_page(q):
+            tile = keep.tile([P, T2], F32, name="page%d" % q)
+            nc.sync.dma_start(tile[:], page0[q * P : (q + 1) * P, :])
+            return tile
+
+        def load_chunk(name, w, chunk):
+            return [load_weight(name, w, chunk, a) for a in range(PASSES)]
+
+        offs_t = load_list("offs_t", offs)
+        tab_w = [load_words("tab_w0", tab_words[0])]
+        load_scale_rows(tab_planes, tab_scales, nc.sync)
+        w2_raw = [load_chunk("w2", w2, 0)]
+        tab_w.append(load_words("tab_w1", tab_words[1]))
+        load_scale_rows(w3_planes, w3_scales, nc.sync)
+        w1_raw = [load_chunk("w1", w1, 0)]
+        w3_w = keep.tile([P, PASSES * 2 * H], U8, name="w3_w", align_bytes=64)
+        nc.sync.dma_start(
+            w3_w[:].bitcast(I32).rearrange("p (a c) -> p a c", a=PASSES),
+            w3_words.bitcast(I32).rearrange("a p c -> p a c"),
+        )
+        wgs_t = keep.tile([P, S], F32, name="wgs_t", tag="wgs_t", align_bytes=64)
+        nc.sync.dma_start(wgs_t[:], wgs)
+        offs3_t = load_list("offs3_t", offs3)
+        page = [load_page(0)]
+        w2_raw.append(load_chunk("w2", w2, 1))
+        w1_raw.append(load_chunk("w1", w1, 1))
+        page.append(load_page(1))
+        w4_raw = [load_chunk("w4", w4, 0), load_chunk("w4", w4, 1)]
+        page.append(load_page(2))
+        page.append(load_page(3))
+        offs2_t = load_list("offs2_t", offs2)
+        tab2_w = load_words("tab2_w", tab2_words[0])
+        load_scale_rows(tab2_planes, tab2_scales, nc.sync)
+        pos1_t = load_list("pos1_t", pos1)
+        pos2_t = load_list("pos2_t", pos2)
+        orbit_cols = keep.tile([P, S2 // P], F32, name="orbit_cols")
+        with nc.allow_non_contiguous_dma(reason="one value of orbit to a partition"):
+            nc.sync.dma_start(orbit_cols[:], orbit.rearrange("(c p) -> p c", p=P))
+        w4_raw.append(load_chunk("w4", w4, 2))
+        w4_raw.append(load_chunk("w4", w4, 3))
+
+        v_w, v_s = [], []
+        for a in range(PASSES):
+            words = keep.tile([P, S], U32, name="v_w%d" % a, align_bytes=64)
+            plane = keep.tile([P, S], U8, name="v_s%d" % a, align_bytes=64)
+            nc.vector.tensor_copy(words[:], tab_w[a][:].indirect(offs_t[:]))
+            nc.vector.tensor_copy(plane[:], tab_planes[:, a * T : (a + 1) * T].indirect(offs_t[:]))
+            v_w.append(words)
+            v_s.append(plane)
+
+        def product_with_v(acc, codes, scales, col):
+            for a in range(PASSES):
+                cols = slice(a * CHUNK + col, a * CHUNK + col + P)
+                nc.tensor.matmul_mx(
+                    out=acc[:], lhsT=codes[:, cols].bitcast(FP8X4), lhsT_scale=scales[:, cols],
+                    rhs=v_w[a][:].bitcast(FP8X4), rhs_scale=v_s[a][:],
+                    start=(a == 0), stop=(a == PASSES - 1),
+                )
+
+        w1_q, w2_q, w4_q = [], [], []
+
+        def work(name, q, dtype, tag=None):
+            return keep.tile([P, S], dtype, name=name, tag=tag or "%s%d" % (name, q % 2), align_bytes=64)
+
+        def first_products(q, banks, whole_tag=None, part_tag=None, sine_tag=None, tanh_tag=None, diff_tag=None):
+            chunk, col = divmod(q * P, CHUNK)
+            p2, p1, p3 = [bank(b, [P, S]) for b in banks]
+            product_with_v(p2, w2_q[chunk][0], w2_q[chunk][1], col)
+            product_with_v(p1, w1_q[chunk][0], w1_q[chunk][1], col)
+            for a in range(PASSES):
+                nc.tensor.matmul_mx(
+                    out=p3[:],
+                    lhsT=w3_w[:, 2 * (a * H + q * P) : 2 * (a * H + (q + 1) * P)].bitcast(FP4X4),
+                    lhsT_scale=w3_planes[:, a * H + q * P : a * H + (q + 1) * P],
+                    rhs=v_w[a][:].bitcast(FP8X4), rhs_scale=v_s[a][:],
+                    start=(a == 0), stop=(a == PASSES - 1),
+                )
+            whole = work("whole", q, I32, whole_tag)
+            nc.vector.tensor_scalar(whole[:], p2[:], 1.0 / TURN, None, ALU.mult)
+            part = work("part", q, F32, part_tag)
+            nc.vector.scalar_tensor_tensor(part[:], p2[:], 1.0 / TURN, whole[:], ALU.mult, ALU.subtract)
+            sine = work("sine", q, F32, sine_tag)
+            nc.scalar.activation(sine[:], part[:], ACT.Sin, scale=TURN)
+            tanh = work("tanh", q, F32, tanh_tag)
+            nc.scalar.activation(tanh[:], p1[:], ACT.Tanh)
+            diff = work("diff", q, F32, diff_tag)
+            nc.vector.tensor_tensor(diff[:], tanh[:], sine[:], ALU.subtract)
+            return diff, p3
+
+        def renew(q, diff, p3, h_tag=None):
+            h = work("h", q, F32, h_tag)
+            nc.vector.tensor_tensor(h[:], p3[:], diff[:], ALU.mult)
+            nc.vector.tensor_tensor(page[q][:].indirect(offs3_t[:]), h[:], wgs_t[:], ALU.mult)
+
+        def turn(q, banks):
+            for half in range(2):
+                flip = bank(banks[half], [P, 4, P])
+                for nb in range(4):
+                    n0 = half * BANK + nb * P
+                    nc.tensor.transpose(flip[:, nb, :], page[q][:, n0 : n0 + P], identity[:])
+                dst = turned[half][:].rearrange("n (b u p e) -> n b u p e", b=4, u=2, e=2)
+                nc.scalar.copy(
+                    dst[:, :, :, 32 * q : 32 * (q + 1), :],
+                    flip[:].rearrange("n b (p u e) -> n b u p e", u=2, e=2),
+                )
+
+        direct = []
+
+        def score_directly(mb, b):
+            chunk, col = divmod(mb * P, CHUNK)
+            f = bank(b, [P, S])
+            product_with_v(f, w4_q[chunk][0], w4_q[chunk][1], col)
+            tile = keep.tile([P, S], F32, name="direct", tag="direct%d" % (mb % 3))
+            nc.scalar.activation(tile[:], f[:], ACT.Identity, bias=orbit_cols[:, mb : mb + 1])
+            direct.append(tile)
+
+        w2_q.append(quantise_weight("w2_0", w2_raw[0], "mix0"))
+        w1_q.append(quantise_weight("w1_0", w1_raw[0], "mix1"))
+        renew(0, *first_products(0, (0, 2, 4), sine_tag="w1_raw01", tanh_tag="mix2"))
+        products = first_products(1, (1, 3, 5), part_tag="mix1")
+        w2_q.append(quantise_weight("w2_1", w2_raw[1], "mix2"))
+        w1_q.append(quantise_weight("w1_1", w1_raw[1], "w2_raw11"))
+        renew(1, *products, h_tag="w2_raw11")
+        w4_mixed = [interleaved("w1_raw11"), interleaved("w4_raw01")]
+        for chunk in range(2):
+            cast_weight(w4_raw[chunk], w4_mixed[chunk])
+        renew(2, *first_products(2, (7, 6, 4), whole_tag="diff1", sine_tag="w4_raw11"))
+        renew(3, *first_products(3, (0, 2, 5), whole_tag="w2_raw11", sine_tag="w4_raw11", diff_tag="diff3"))
+        w4_q.append(quantise("w4_0", w4_mixed[0], "w2_raw11"))
+        w4_q.append(quantise("w4_1", w4_mixed[1], "diff1"))
+        turned = [interleaved("w4_raw01"), interleaved("w1_raw11")]
+        turn(0, (7, 7))
+        turn(1, (4, 7))
+        turn(2, (0, 4))
+        turn(3, (5, 7))
+
+        v2_w, v2_s = [], []
+
+        def pick_orbits(half, tags):
+            words = keep.tile([P, S2 // 2], U32, name="v2_w", tag=tags[0], align_bytes=64)
+            plane = keep.tile([P, S2 // 2], U8, name="v2_s", tag=tags[1], align_bytes=64)
+            picks = offs2_t[:, 32 * half : 32 * (half + 1)]
+            nc.vector.tensor_copy(words[:], tab2_w[:].indirect(picks))
+            nc.vector.tensor_copy(plane[:], tab2_planes[:].indirect(picks))
+            v2_w.append(words)
+            v2_s.append(plane)
+
+        pick_orbits(0, ("h1", "wgs_t"))
+        page_q = []
+        for half in range(2):
+            pairs = turned[half][:].bitcast(F32).rearrange("n (b u p) -> n b u p", b=4, u=2)
+            grouped = interleaved("mix%d" % half)
+            grouped_pairs = grouped[:].bitcast(F32).rearrange("p (b n u) -> p b n u", b=4, u=2)
+            for two in range(2):
+                back = bank((6, 2, 0, 4)[2 * half + two], [P, 2, 2, P])
+                for b in range(2):
+                    for u in range(2):
+                        nc.tensor.transpose(back[:, b, u, :], pairs[:, 2 * two + b, u, :], identity[:])
+                nc.scalar.copy(grouped_pairs[:, 2 * two : 2 * two + 2, :, :], back[:].rearrange("p b u n -> p b n u"))
+            page_q.append(quantise("page_q%d" % half, grouped, "page_q%d" % half))
+
+        pick_orbits(1, ("mix1", "mix0"))
+
+        for mb in range(S2 // P):
+            group, col = divmod(mb * P, S2 // 2)
+            scores = ring3.tile([P, T2], F32, name="scores")
+            pair = ((1, 3), (5, 7), (6, 2))[mb % 3]
+            for half in range(2):
+                acc = bank(pair[half], [P, BANK])
+                nc.tensor.matmul_mx(
+                    out=acc[:],
+                    lhsT=v2_w[group][:, col : col + P].bitcast(FP8X4), lhsT_scale=v2_s[group][:, col : col + P],
+                    rhs=page_q[half][0][:].bitcast(FP8X4), rhs_scale=page_q[half][1][:],
+                    start=True, stop=True,
+                )
+                nc.scalar.copy(scores[:, half * BANK : (half + 1) * BANK], acc[:])
+            score_directly(mb, pair[1])
+            second_tag = ("mix2", "w4_raw01")[mb] if mb < 2 else "second%d" % (mb % 2)
+            second = keep.tile([P, PAIRS], F32, name="second", tag=second_tag, align_bytes=64)
+            nc.vector.tensor_copy(second[:], scores[:].indirect(pos2_t[:]))
+            gap_tag = "late%d" % mb if mb in (1, 2) else "gap%d" % (mb % 2)
+            gap = keep.tile([P, PAIRS], F32, name="gap", tag=gap_tag, align_bytes=64)
+            nc.vector.tensor_tensor(gap[:], scores[:].indirect(pos1_t[:]), second[:], ALU.subtract)
+            result = ring3.tile([P, PAIRS], F32, name="result")
+            nc.vector.scalar_tensor_tensor(result[:], gap[:], orbit_cols[:, mb : mb + 1], direct[mb][:], ALU.add, ALU.max)
+            if mb in (1, 2):
+                chunk = 1 + mb
+                w4_q.append(quantise_weight("w4_%d" % chunk, w4_raw[chunk], ("mix2", "w4_raw01")[chunk - 2], gap_tag))
+            nc.sync.dma_start(out[mb * P : (mb + 1) * P, :], result[:])

@@ -26,6 +26,7 @@ CHUNK = 256
 BANK = 512
 QUADS = 4
 TURN = 2.0 * math.pi
+LIFT = 1.5 * 2.0**23
 
 
 def tile_list_tracklet_orbit_features_kernel(
@@ -35,6 +36,7 @@ def tile_list_tracklet_orbit_features_kernel(
     nc = tc.nc
     with ExitStack() as ctx:
         keep = ctx.enter_context(tc.tile_pool(name="keep", bufs=1))
+        ring4 = ctx.enter_context(tc.tile_pool(name="ring4", bufs=4))
         ring3 = ctx.enter_context(tc.tile_pool(name="ring3", bufs=3))
         ring2 = ctx.enter_context(tc.tile_pool(name="ring2", bufs=2))
         psum = ctx.enter_context(tc.psum_pool(name="psum", bufs=1))
@@ -47,8 +49,8 @@ def tile_list_tracklet_orbit_features_kernel(
             nc.sync.dma_start(tile[:], src)
             return tile
 
-        def interleaved(tag):
-            return keep.tile([P, BANK * PACK], BF16, name=tag, tag=tag, align_bytes=64)
+        def interleaved(tag, words=BANK):
+            return keep.tile([P, words * PACK], BF16, name=tag, tag=tag, align_bytes=64)
 
         def cleared_plane(name, src, clearer):
             plane = keep.tile([P, src.shape[0] * src.shape[2]], U8, name=name, align_bytes=64)
@@ -87,8 +89,9 @@ def tile_list_tracklet_orbit_features_kernel(
                 nc.scalar.copy(dst, src)
 
         def quantise(name, grouped, codes_tag):
-            codes = keep.tile([P, BANK], U32, name=name + "_codes", tag=codes_tag, align_bytes=64)
-            scales = keep.tile([P, BANK], U8, name=name + "_scales", align_bytes=64)
+            words = grouped.shape[1] // PACK
+            codes = keep.tile([P, words], U32, name=name + "_codes", tag=codes_tag, align_bytes=64)
+            scales = keep.tile([P, words], U8, name=name + "_scales", align_bytes=64)
             nc.vector.quantize_mx(out=codes[:].bitcast(FP8X4), scales=scales[:], in_=grouped[:])
             return codes, scales
 
@@ -109,8 +112,8 @@ def tile_list_tracklet_orbit_features_kernel(
         def load_chunk(name, w, chunk):
             return [load_weight(name, w, chunk, a) for a in range(PASSES)]
 
-        offs_t = load_list("offs_t", offs)
         tab_w = [load_words("tab_w0", tab_words[0])]
+        offs_t = load_list("offs_t", offs)
         load_scale_rows(tab_planes, tab_scales, nc.sync)
         w2_raw = [load_chunk("w2", w2, 0)]
         tab_w.append(load_words("tab_w1", tab_words[1]))
@@ -128,8 +131,8 @@ def tile_list_tracklet_orbit_features_kernel(
         w2_raw.append(load_chunk("w2", w2, 1))
         w1_raw.append(load_chunk("w1", w1, 1))
         page.append(load_page(1))
-        w4_raw = [load_chunk("w4", w4, 0), load_chunk("w4", w4, 1)]
         page.append(load_page(2))
+        w4_raw = [load_chunk("w4", w4, 0)]
         page.append(load_page(3))
         offs2_t = load_list("offs2_t", offs2)
         tab2_w = load_words("tab2_w", tab2_words[0])
@@ -139,8 +142,8 @@ def tile_list_tracklet_orbit_features_kernel(
         orbit_cols = keep.tile([P, S2 // P], F32, name="orbit_cols")
         with nc.allow_non_contiguous_dma(reason="one value of orbit to a partition"):
             nc.sync.dma_start(orbit_cols[:], orbit.rearrange("(c p) -> p c", p=P))
-        w4_raw.append(load_chunk("w4", w4, 2))
-        w4_raw.append(load_chunk("w4", w4, 3))
+        for chunk in range(1, S2 // CHUNK):
+            w4_raw.append(load_chunk("w4", w4, chunk))
 
         v_w, v_s = [], []
         for a in range(PASSES):
@@ -165,7 +168,7 @@ def tile_list_tracklet_orbit_features_kernel(
         def work(name, q, dtype, tag=None):
             return keep.tile([P, S], dtype, name=name, tag=tag or "%s%d" % (name, q % 2), align_bytes=64)
 
-        def first_products(q, banks, whole_tag=None, part_tag=None, sine_tag=None, tanh_tag=None, diff_tag=None):
+        def first_products(q, banks):
             chunk, col = divmod(q * P, CHUNK)
             p2, p1, p3 = [bank(b, [P, S]) for b in banks]
             product_with_v(p2, w2_q[chunk][0], w2_q[chunk][1], col)
@@ -178,17 +181,30 @@ def tile_list_tracklet_orbit_features_kernel(
                     rhs=v_w[a][:].bitcast(FP8X4), rhs_scale=v_s[a][:],
                     start=(a == 0), stop=(a == PASSES - 1),
                 )
-            whole = work("whole", q, I32, whole_tag)
+            return p1, p2, p3
+
+        def turns_on_vector(q, p2):
+            whole = work("whole", q, I32)
             nc.vector.tensor_scalar(whole[:], p2[:], 1.0 / TURN, None, ALU.mult)
+            return whole
+
+        def turns_on_scalar(q, p2):
+            lifted = work("lifted", q, U32)
+            nc.scalar.activation(lifted[:], p2[:], ACT.Copy, scale=1.0 / TURN, bias=LIFT)
+            whole = work("whole", q, F32)
+            nc.scalar.activation(whole[:], lifted[:], ACT.Copy, bias=-LIFT)
+            return whole
+
+        def difference(q, p1, p2, whole, part_tag=None, sine_tag=None, tanh_tag=None):
             part = work("part", q, F32, part_tag)
             nc.vector.scalar_tensor_tensor(part[:], p2[:], 1.0 / TURN, whole[:], ALU.mult, ALU.subtract)
             sine = work("sine", q, F32, sine_tag)
             nc.scalar.activation(sine[:], part[:], ACT.Sin, scale=TURN)
             tanh = work("tanh", q, F32, tanh_tag)
             nc.scalar.activation(tanh[:], p1[:], ACT.Tanh)
-            diff = work("diff", q, F32, diff_tag)
+            diff = work("diff", q, F32)
             nc.vector.tensor_tensor(diff[:], tanh[:], sine[:], ALU.subtract)
-            return diff, p3
+            return diff
 
         def renew(q, diff, p3, h_tag=None):
             h = work("h", q, F32, h_tag)
@@ -208,32 +224,39 @@ def tile_list_tracklet_orbit_features_kernel(
                 )
 
         direct = []
+        second_tags = ["%s_raw%d%d" % (name, chunk, a) for name in ("w2", "w1") for chunk in range(2) for a in range(PASSES)]
 
-        def score_directly(mb, b):
+        def score_directly(mb, b, tile):
             chunk, col = divmod(mb * P, CHUNK)
             f = bank(b, [P, S])
             product_with_v(f, w4_q[chunk][0], w4_q[chunk][1], col)
-            tile = keep.tile([P, S], F32, name="direct", tag="direct%d" % (mb % 3))
-            nc.scalar.activation(tile[:], f[:], ACT.Identity, bias=orbit_cols[:, mb : mb + 1])
+            nc.scalar.activation(tile, f[:], ACT.Identity, bias=orbit_cols[:, mb : mb + 1])
             direct.append(tile)
 
         w2_q.append(quantise_weight("w2_0", w2_raw[0], "mix0"))
         w1_q.append(quantise_weight("w1_0", w1_raw[0], "mix1"))
-        renew(0, *first_products(0, (0, 2, 4), sine_tag="w1_raw01", tanh_tag="mix2"))
-        products = first_products(1, (1, 3, 5), part_tag="mix1")
-        w2_q.append(quantise_weight("w2_1", w2_raw[1], "mix2"))
-        w1_q.append(quantise_weight("w1_1", w1_raw[1], "w2_raw11"))
-        renew(1, *products, h_tag="w2_raw11")
-        w4_mixed = [interleaved("w1_raw11"), interleaved("w4_raw01")]
-        for chunk in range(2):
-            cast_weight(w4_raw[chunk], w4_mixed[chunk])
-        renew(2, *first_products(2, (7, 6, 4), whole_tag="diff1", sine_tag="w4_raw11"))
-        renew(3, *first_products(3, (0, 2, 5), whole_tag="w2_raw11", sine_tag="w4_raw11", diff_tag="diff3"))
-        w4_q.append(quantise("w4_0", w4_mixed[0], "w2_raw11"))
-        w4_q.append(quantise("w4_1", w4_mixed[1], "diff1"))
-        turned = [interleaved("w4_raw01"), interleaved("w1_raw11")]
+        p1, p2, p3 = first_products(0, (0, 2, 4))
+        renew(0, difference(0, p1, p2, turns_on_vector(0, p2), sine_tag="w1_raw01", tanh_tag="wide"), p3)
+        p1, p2, p3 = first_products(1, (1, 3, 5))
+        diff = difference(1, p1, p2, turns_on_vector(1, p2), part_tag="mix1")
+        both = interleaved("wide", 2 * BANK)
+        cast_weight(w2_raw[1], both[:, : BANK * PACK])
+        cast_weight(w1_raw[1], both[:, BANK * PACK :])
+        codes, scales = quantise("w21_1", both, "w21_1")
+        w2_q.append((codes[:, :BANK], scales[:, :BANK]))
+        w1_q.append((codes[:, BANK:], scales[:, BANK:]))
+        renew(1, diff, p3, h_tag="wide")
+        late = [first_products(2, (7, 6, 4)), first_products(3, (0, 2, 5))]
+        wholes = [turns_on_scalar(2 + i, late[i][1]) for i in range(2)]
+        diffs = [difference(2 + i, late[i][0], late[i][1], wholes[i], part_tag=("lifted1", "wide")[i]) for i in range(2)]
+        renew(2, diffs[0], late[0][2])
+        w4_mixed = interleaved("sine0")
+        cast_weight(w4_raw[0], w4_mixed)
+        renew(3, diffs[1], late[1][2], h_tag="w4_raw01")
+        w4_q.append(quantise("w4_0", w4_mixed, "w4_0"))
+        turned = [interleaved("wide"), interleaved("turned1")]
         turn(0, (7, 7))
-        turn(1, (4, 7))
+        turn(1, (0, 7))
         turn(2, (0, 4))
         turn(3, (5, 7))
 
@@ -248,7 +271,7 @@ def tile_list_tracklet_orbit_features_kernel(
             v2_w.append(words)
             v2_s.append(plane)
 
-        pick_orbits(0, ("h1", "wgs_t"))
+        pick_orbits(0, ("w4_raw01", "wgs_t"))
         page_q = []
         for half in range(2):
             pairs = turned[half][:].bitcast(F32).rearrange("n (b u p) -> n b u p", b=4, u=2)
@@ -262,14 +285,15 @@ def tile_list_tracklet_orbit_features_kernel(
                 nc.scalar.copy(grouped_pairs[:, 2 * two : 2 * two + 2, :, :], back[:].rearrange("p b u n -> p b n u"))
             page_q.append(quantise("page_q%d" % half, grouped, "page_q%d" % half))
 
-        pick_orbits(1, ("mix1", "mix0"))
+        pick_orbits(1, ("wide", "mix1"))
 
-        for mb in range(S2 // P):
+        score_banks = ((1, 3), (3, 5), (5, 7), (7, 6), (1, 3), (5, 2), (0, 4), (7, 6))
+
+        def score_page(mb):
             group, col = divmod(mb * P, S2 // 2)
-            scores = ring3.tile([P, T2], F32, name="scores")
-            pair = ((1, 3), (5, 7), (6, 2))[mb % 3]
+            scores = ring4.tile([P, T2], F32, name="scores")
             for half in range(2):
-                acc = bank(pair[half], [P, BANK])
+                acc = bank(score_banks[mb][half], [P, BANK])
                 nc.tensor.matmul_mx(
                     out=acc[:],
                     lhsT=v2_w[group][:, col : col + P].bitcast(FP8X4), lhsT_scale=v2_s[group][:, col : col + P],
@@ -277,16 +301,38 @@ def tile_list_tracklet_orbit_features_kernel(
                     start=True, stop=True,
                 )
                 nc.scalar.copy(scores[:, half * BANK : (half + 1) * BANK], acc[:])
-            score_directly(mb, pair[1])
-            second_tag = ("mix2", "w4_raw01")[mb] if mb < 2 else "second%d" % (mb % 2)
-            second = keep.tile([P, PAIRS], F32, name="second", tag=second_tag, align_bytes=64)
-            nc.vector.tensor_copy(second[:], scores[:].indirect(pos2_t[:]))
-            gap_tag = "late%d" % mb if mb in (1, 2) else "gap%d" % (mb % 2)
-            gap = keep.tile([P, PAIRS], F32, name="gap", tag=gap_tag, align_bytes=64)
-            nc.vector.tensor_tensor(gap[:], scores[:].indirect(pos1_t[:]), second[:], ALU.subtract)
+            return scores
+
+        def finish(mb, gap):
             result = ring3.tile([P, PAIRS], F32, name="result")
-            nc.vector.scalar_tensor_tensor(result[:], gap[:], orbit_cols[:, mb : mb + 1], direct[mb][:], ALU.add, ALU.max)
-            if mb in (1, 2):
-                chunk = 1 + mb
-                w4_q.append(quantise_weight("w4_%d" % chunk, w4_raw[chunk], ("mix2", "w4_raw01")[chunk - 2], gap_tag))
+            nc.vector.scalar_tensor_tensor(result[:], gap[:], orbit_cols[:, mb : mb + 1], direct[mb], ALU.add, ALU.max)
             nc.sync.dma_start(out[mb * P : (mb + 1) * P, :], result[:])
+
+        gaps = []
+        for chunk in range(S2 // CHUNK):
+            pair = (2 * chunk, 2 * chunk + 1)
+            scores = [score_page(mb) for mb in pair]
+            seconds = []
+            for i, mb in enumerate(pair):
+                second = keep.tile([P, PAIRS], F32, name="second", tag=second_tags[mb], align_bytes=64)
+                nc.vector.tensor_copy(second[:], scores[i][:].indirect(pos2_t[:]))
+                seconds.append(second)
+            if chunk > 0:
+                w4_q.append(quantise("w4_%d" % chunk, w4_mixed, "w4_%d" % chunk))
+                two = keep.tile([P, 2 * S], F32, name="two", tag="w4_raw%d1" % chunk, align_bytes=64)
+                for i, mb in enumerate(pair):
+                    score_directly(mb - 2, score_banks[pair[1]][i], two[:, i * S : (i + 1) * S])
+                for mb in pair:
+                    finish(mb - 2, gaps[mb - 2])
+            for i, mb in enumerate(pair):
+                gap = ring2.tile([P, PAIRS], F32, name="gap")
+                nc.vector.tensor_tensor(gap[:], scores[i][:].indirect(pos1_t[:]), seconds[i][:], ALU.subtract)
+                gaps.append(gap)
+            if chunk + 1 < S2 // CHUNK:
+                w4_mixed = interleaved(second_tags[pair[0]])
+                cast_weight(w4_raw[chunk + 1], w4_mixed)
+        two = keep.tile([P, 2 * S], F32, name="two", tag="w4_raw00", align_bytes=64)
+        for i, mb in enumerate(pair):
+            score_directly(mb, score_banks[0][i], two[:, i * S : (i + 1) * S])
+        for mb in pair:
+            finish(mb, gaps[mb])

@@ -22,11 +22,13 @@ P = 128
 PACK = 4
 K_PASS = P * PACK
 PASSES = K // K_PASS
-CHUNK = 256
 BANK = 512
+CHUNK = 256
 QUADS = 4
 TURN = 2.0 * math.pi
 LIFT = 1.5 * 2.0**23
+
+SCORE_BANKS = ((1, 3), (3, 2), (2, 7), (7, 0), (1, 3), (4, 5), (0, 2), (7, 6))
 
 
 def tile_list_tracklet_orbit_features_kernel(
@@ -36,32 +38,37 @@ def tile_list_tracklet_orbit_features_kernel(
     nc = tc.nc
     with ExitStack() as ctx:
         keep = ctx.enter_context(tc.tile_pool(name="keep", bufs=1))
-        ring4 = ctx.enter_context(tc.tile_pool(name="ring4", bufs=4))
-        ring3 = ctx.enter_context(tc.tile_pool(name="ring3", bufs=3))
-        ring2 = ctx.enter_context(tc.tile_pool(name="ring2", bufs=2))
+        scores_pool = ctx.enter_context(tc.tile_pool(name="scores_pool", bufs=4))
+        result_pool = ctx.enter_context(tc.tile_pool(name="result_pool", bufs=3))
+        gap_pool = ctx.enter_context(tc.tile_pool(name="gap_pool", bufs=2))
         psum = ctx.enter_context(tc.psum_pool(name="psum", bufs=1))
 
         def bank(b, shape):
             return psum.tile(shape, F32, name="bank%d" % b, tag="bank%d" % b)
+
+        def raw_tag(name, chunk, a):
+            return "%s_raw%d%d" % (name, chunk, a)
+
+        def interleaved(tag, words=BANK):
+            return keep.tile([P, words * PACK], BF16, name=tag, tag=tag, align_bytes=64)
+
+        def work(name, q, dtype, tag=None):
+            return keep.tile([P, S], dtype, name=name, tag=tag or "%s%d" % (name, q % 2), align_bytes=64)
 
         def load_list(name, src):
             tile = keep.tile(list(src.shape), U16, name=name)
             nc.sync.dma_start(tile[:], src)
             return tile
 
-        def interleaved(tag, words=BANK):
-            return keep.tile([P, words * PACK], BF16, name=tag, tag=tag, align_bytes=64)
+        def cleared_planes(name, src, engine):
+            planes = keep.tile([P, src.shape[0] * src.shape[2]], U8, name=name, align_bytes=64)
+            engine.memset(planes[:].bitcast(I32), 0)
+            return planes
 
-        def cleared_plane(name, src, clearer):
-            plane = keep.tile([P, src.shape[0] * src.shape[2]], U8, name=name, align_bytes=64)
-            clearer.memset(plane[:].bitcast(I32), 0)
-            return plane
-
-        def load_scale_rows(plane, src, queue):
-            passes = src.shape[0]
+        def load_scale_rows(planes, src):
             for quad in range(QUADS):
-                queue.dma_start(
-                    plane[32 * quad : 32 * quad + 4, :].bitcast(I32).rearrange("r (a c) -> r a c", a=passes),
+                nc.sync.dma_start(
+                    planes[32 * quad : 32 * quad + 4, :].bitcast(I32).rearrange("r (a c) -> r a c", a=src.shape[0]),
                     src[:, 4 * quad : 4 * quad + 4, :].bitcast(I32).rearrange("a r c -> r a c"),
                 )
 
@@ -70,54 +77,35 @@ def tile_list_tracklet_orbit_features_kernel(
             nc.sync.dma_start(tile[:].bitcast(I32), src.rearrange("p t i -> p (t i)").bitcast(I32))
             return tile
 
-        def load_weight(name, w, chunk, a):
-            raw = keep.tile([P, PACK, CHUNK], F32, name="raw", tag="%s_raw%d%d" % (name, chunk, a), align_bytes=64)
-            rows = w[a * K_PASS : (a + 1) * K_PASS, chunk * CHUNK : (chunk + 1) * CHUNK]
-            nc.sync.dma_start(raw[:], rows.rearrange("(p j) c -> p j c", j=PACK))
-            return raw
-
-        def quantise_weight(name, raw_passes, grouped_tag, codes_tag=None):
-            grouped = interleaved(grouped_tag)
-            cast_weight(raw_passes, grouped)
-            return quantise(name, grouped, codes_tag or name)
-
-        def cast_weight(raw_passes, grouped):
+        def load_chunk(name, w, chunk):
+            tiles = []
             for a in range(PASSES):
-                dst = grouped[:, a * CHUNK * PACK : (a + 1) * CHUNK * PACK]
-                dst = dst.rearrange("p (c i t) -> p c t i", i=4, t=PACK)
-                src = raw_passes[a][:].rearrange("p t (c i) -> p c t i", i=4)
-                nc.scalar.copy(dst, src)
-
-        def quantise(name, grouped, codes_tag):
-            words = grouped.shape[1] // PACK
-            codes = keep.tile([P, words], U32, name=name + "_codes", tag=codes_tag, align_bytes=64)
-            scales = keep.tile([P, words], U8, name=name + "_scales", align_bytes=64)
-            nc.vector.quantize_mx(out=codes[:].bitcast(FP8X4), scales=scales[:], in_=grouped[:])
-            return codes, scales
-
-        tab_planes = cleared_plane("tab_planes", tab_scales, nc.vector)
-        warm = keep.tile([P, 2], F32, name="warm")
-        nc.vector.memset(warm[:, 0:1], 0.0)
-        nc.scalar.activation(warm[:, 1:2], warm[:, 0:1], ACT.Silu)
-        w3_planes = cleared_plane("w3_planes", w3_scales, nc.gpsimd)
-        tab2_planes = cleared_plane("tab2_planes", tab2_scales, nc.gpsimd)
-        identity = keep.tile([P, P], F32, name="identity")
-        make_identity(nc, identity[:])
+                raw = keep.tile([P, PACK, CHUNK], F32, name="raw", tag=raw_tag(name, chunk, a), align_bytes=64)
+                rows = w[a * K_PASS : (a + 1) * K_PASS, chunk * CHUNK : (chunk + 1) * CHUNK]
+                nc.sync.dma_start(raw[:], rows.rearrange("(p t) c -> p t c", t=PACK))
+                tiles.append(raw)
+            return tiles
 
         def load_page(q):
             tile = keep.tile([P, T2], F32, name="page%d" % q)
             nc.sync.dma_start(tile[:], page0[q * P : (q + 1) * P, :])
             return tile
 
-        def load_chunk(name, w, chunk):
-            return [load_weight(name, w, chunk, a) for a in range(PASSES)]
+        tab_planes = cleared_planes("tab_planes", tab_scales, nc.vector)
+        warm = keep.tile([P, 2], F32, name="warm")
+        nc.vector.memset(warm[:, 0:1], 0.0)
+        nc.scalar.activation(warm[:, 1:2], warm[:, 0:1], ACT.Silu)
+        w3_planes = cleared_planes("w3_planes", w3_scales, nc.gpsimd)
+        tab2_planes = cleared_planes("tab2_planes", tab2_scales, nc.gpsimd)
+        identity = keep.tile([P, P], F32, name="identity")
+        make_identity(nc, identity[:])
 
         tab_w = [load_words("tab_w0", tab_words[0])]
         offs_t = load_list("offs_t", offs)
-        load_scale_rows(tab_planes, tab_scales, nc.sync)
+        load_scale_rows(tab_planes, tab_scales)
         w2_raw = [load_chunk("w2", w2, 0)]
         tab_w.append(load_words("tab_w1", tab_words[1]))
-        load_scale_rows(w3_planes, w3_scales, nc.sync)
+        load_scale_rows(w3_planes, w3_scales)
         w1_raw = [load_chunk("w1", w1, 0)]
         w3_w = keep.tile([P, PASSES * 2 * H], U8, name="w3_w", align_bytes=64)
         nc.sync.dma_start(
@@ -136,14 +124,34 @@ def tile_list_tracklet_orbit_features_kernel(
         page.append(load_page(3))
         offs2_t = load_list("offs2_t", offs2)
         tab2_w = load_words("tab2_w", tab2_words[0])
-        load_scale_rows(tab2_planes, tab2_scales, nc.sync)
+        load_scale_rows(tab2_planes, tab2_scales)
         pos1_t = load_list("pos1_t", pos1)
         pos2_t = load_list("pos2_t", pos2)
         orbit_cols = keep.tile([P, S2 // P], F32, name="orbit_cols")
-        with nc.allow_non_contiguous_dma(reason="one value of orbit to a partition"):
+        with nc.allow_non_contiguous_dma(reason="one value of orbit to a partition and row block"):
             nc.sync.dma_start(orbit_cols[:], orbit.rearrange("(c p) -> p c", p=P))
         for chunk in range(1, S2 // CHUNK):
             w4_raw.append(load_chunk("w4", w4, chunk))
+
+        def round_weight(raw_passes, grouped):
+            for a in range(PASSES):
+                dst = grouped[:, a * CHUNK * PACK : (a + 1) * CHUNK * PACK]
+                nc.scalar.copy(
+                    dst.rearrange("p (c i t) -> p c t i", i=4, t=PACK),
+                    raw_passes[a][:].rearrange("p t (c i) -> p c t i", i=4),
+                )
+
+        def quantise(name, grouped, pieces=1):
+            words = grouped.shape[1] // PACK
+            codes = keep.tile([P, words], U32, name=name + "_codes", align_bytes=64)
+            scales = keep.tile([P, words], U8, name=name + "_scales", align_bytes=64)
+            step = words // pieces
+            for w0 in range(0, words, step):
+                nc.vector.quantize_mx(
+                    out=codes[:, w0 : w0 + step].bitcast(FP8X4), scales=scales[:, w0 : w0 + step],
+                    in_=grouped[:, PACK * w0 : PACK * (w0 + step)],
+                )
+            return codes, scales
 
         v_w, v_s = [], []
         for a in range(PASSES):
@@ -154,7 +162,10 @@ def tile_list_tracklet_orbit_features_kernel(
             v_w.append(words)
             v_s.append(plane)
 
-        def product_with_v(acc, codes, scales, col):
+        def fp8_product(chunks, block, b):
+            chunk, col = divmod(block * P, CHUNK)
+            codes, scales = chunks[chunk]
+            acc = bank(b, [P, S])
             for a in range(PASSES):
                 cols = slice(a * CHUNK + col, a * CHUNK + col + P)
                 nc.tensor.matmul_mx(
@@ -162,26 +173,19 @@ def tile_list_tracklet_orbit_features_kernel(
                     rhs=v_w[a][:].bitcast(FP8X4), rhs_scale=v_s[a][:],
                     start=(a == 0), stop=(a == PASSES - 1),
                 )
+            return acc
 
-        w1_q, w2_q, w4_q = [], [], []
-
-        def work(name, q, dtype, tag=None):
-            return keep.tile([P, S], dtype, name=name, tag=tag or "%s%d" % (name, q % 2), align_bytes=64)
-
-        def first_products(q, banks):
-            chunk, col = divmod(q * P, CHUNK)
-            p2, p1, p3 = [bank(b, [P, S]) for b in banks]
-            product_with_v(p2, w2_q[chunk][0], w2_q[chunk][1], col)
-            product_with_v(p1, w1_q[chunk][0], w1_q[chunk][1], col)
+        def fp4_product(q, b):
+            acc = bank(b, [P, S])
             for a in range(PASSES):
                 nc.tensor.matmul_mx(
-                    out=p3[:],
+                    out=acc[:],
                     lhsT=w3_w[:, 2 * (a * H + q * P) : 2 * (a * H + (q + 1) * P)].bitcast(FP4X4),
                     lhsT_scale=w3_planes[:, a * H + q * P : a * H + (q + 1) * P],
                     rhs=v_w[a][:].bitcast(FP8X4), rhs_scale=v_s[a][:],
                     start=(a == 0), stop=(a == PASSES - 1),
                 )
-            return p1, p2, p3
+            return acc
 
         def turns_on_vector(q, p2):
             whole = work("whole", q, I32)
@@ -195,9 +199,12 @@ def tile_list_tracklet_orbit_features_kernel(
             nc.scalar.activation(whole[:], lifted[:], ACT.Copy, bias=-LIFT)
             return whole
 
-        def difference(q, p1, p2, whole, part_tag=None, sine_tag=None, tanh_tag=None):
-            part = work("part", q, F32, part_tag)
+        def part_turn(q, p2, whole, tag=None):
+            part = work("part", q, F32, tag)
             nc.vector.scalar_tensor_tensor(part[:], p2[:], 1.0 / TURN, whole[:], ALU.mult, ALU.subtract)
+            return part
+
+        def difference(q, p1, part, sine_tag=None, tanh_tag=None):
             sine = work("sine", q, F32, sine_tag)
             nc.scalar.activation(sine[:], part[:], ACT.Sin, scale=TURN)
             tanh = work("tanh", q, F32, tanh_tag)
@@ -211,128 +218,140 @@ def tile_list_tracklet_orbit_features_kernel(
             nc.vector.tensor_tensor(h[:], p3[:], diff[:], ALU.mult)
             nc.vector.tensor_tensor(page[q][:].indirect(offs3_t[:]), h[:], wgs_t[:], ALU.mult)
 
+        mix = [interleaved("mix0")]
+        round_weight(w2_raw[0], mix[0])
+        w2_q = [quantise("w2_0", mix[0])]
+        mix.append(interleaved("mix1"))
+        round_weight(w1_raw[0], mix[1])
+        w1_q = [quantise("w1_0", mix[1], pieces=PASSES)]
+        p2 = [fp8_product(w2_q, 0, 0), fp8_product(w2_q, 1, 1)]
+        p1 = [fp8_product(w1_q, 0, 2), fp8_product(w1_q, 1, 3)]
+        part = part_turn(0, p2[0], turns_on_vector(0, p2[0]))
+        diff = difference(0, p1[0], part, sine_tag=raw_tag("w1", 0, 1), tanh_tag="wide")
+        part = part_turn(1, p2[1], turns_on_vector(1, p2[1]), tag="mix1")
+        renew(0, diff, fp4_product(0, 1))
+        diff = difference(1, p1[1], part)
+        p3 = fp4_product(1, 2)
+
+        wide = interleaved("wide", 2 * BANK)
+        round_weight(w2_raw[1], wide[:, : BANK * PACK])
+        round_weight(w1_raw[1], wide[:, BANK * PACK :])
+        codes, scales = quantise("w21_1", wide)
+        w2_q.append((codes[:, :BANK], scales[:, :BANK]))
+        w1_q.append((codes[:, BANK:], scales[:, BANK:]))
+        renew(1, diff, p3, h_tag="wide")
+
+        p2 = [fp8_product(w2_q, 2, 7), fp8_product(w2_q, 3, 0)]
+        p1 = [fp8_product(w1_q, 2, 6), fp8_product(w1_q, 3, 5)]
+        p3 = [fp4_product(2, 3), fp4_product(3, 2)]
+        wholes = [turns_on_scalar(2 + i, p2[i]) for i in range(2)]
+        diffs = []
+        for i, part_tag in enumerate(("lifted1", "wide")):
+            diffs.append(difference(2 + i, p1[i], part_turn(2 + i, p2[i], wholes[i], part_tag)))
+        renew(2, diffs[0], p3[0])
+        w4_mix = interleaved("sine0")
+        round_weight(w4_raw[0], w4_mix)
+        renew(3, diffs[1], p3[1], h_tag=raw_tag("w4", 0, 1))
+        w4_q = [quantise("w4_0", w4_mix)]
+
+        turned = [interleaved("wide"), interleaved("turned1")]
+
         def turn(q, banks):
             for half in range(2):
                 flip = bank(banks[half], [P, 4, P])
-                for nb in range(4):
-                    n0 = half * BANK + nb * P
-                    nc.tensor.transpose(flip[:, nb, :], page[q][:, n0 : n0 + P], identity[:])
+                for b in range(4):
+                    n0 = half * BANK + b * P
+                    nc.tensor.transpose(flip[:, b, :], page[q][:, n0 : n0 + P], identity[:])
                 dst = turned[half][:].rearrange("n (b u p e) -> n b u p e", b=4, u=2, e=2)
                 nc.scalar.copy(
                     dst[:, :, :, 32 * q : 32 * (q + 1), :],
                     flip[:].rearrange("n b (p u e) -> n b u p e", u=2, e=2),
                 )
 
-        direct = []
-        second_tags = ["%s_raw%d%d" % (name, chunk, a) for name in ("w2", "w1") for chunk in range(2) for a in range(PASSES)]
-
-        def score_directly(mb, b, tile):
-            chunk, col = divmod(mb * P, CHUNK)
-            f = bank(b, [P, S])
-            product_with_v(f, w4_q[chunk][0], w4_q[chunk][1], col)
-            nc.scalar.activation(tile, f[:], ACT.Identity, bias=orbit_cols[:, mb : mb + 1])
-            direct.append(tile)
-
-        w2_q.append(quantise_weight("w2_0", w2_raw[0], "mix0"))
-        w1_q.append(quantise_weight("w1_0", w1_raw[0], "mix1"))
-        p1, p2, p3 = first_products(0, (0, 2, 4))
-        renew(0, difference(0, p1, p2, turns_on_vector(0, p2), sine_tag="w1_raw01", tanh_tag="wide"), p3)
-        p1, p2, p3 = first_products(1, (1, 3, 5))
-        diff = difference(1, p1, p2, turns_on_vector(1, p2), part_tag="mix1")
-        both = interleaved("wide", 2 * BANK)
-        cast_weight(w2_raw[1], both[:, : BANK * PACK])
-        cast_weight(w1_raw[1], both[:, BANK * PACK :])
-        codes, scales = quantise("w21_1", both, "w21_1")
-        w2_q.append((codes[:, :BANK], scales[:, :BANK]))
-        w1_q.append((codes[:, BANK:], scales[:, BANK:]))
-        renew(1, diff, p3, h_tag="wide")
-        late = [first_products(2, (7, 6, 4)), first_products(3, (0, 2, 5))]
-        wholes = [turns_on_scalar(2 + i, late[i][1]) for i in range(2)]
-        diffs = [difference(2 + i, late[i][0], late[i][1], wholes[i], part_tag=("lifted1", "wide")[i]) for i in range(2)]
-        renew(2, diffs[0], late[0][2])
-        w4_mixed = interleaved("sine0")
-        cast_weight(w4_raw[0], w4_mixed)
-        renew(3, diffs[1], late[1][2], h_tag="w4_raw01")
-        w4_q.append(quantise("w4_0", w4_mixed, "w4_0"))
-        turned = [interleaved("wide"), interleaved("turned1")]
         turn(0, (7, 7))
         turn(1, (0, 7))
         turn(2, (0, 4))
-        turn(3, (5, 7))
+        f_pair = [fp8_product(w4_q, 0, 6), fp8_product(w4_q, 1, 5)]
+        turn(3, (2, 7))
 
         v2_w, v2_s = [], []
 
-        def pick_orbits(half, tags):
-            words = keep.tile([P, S2 // 2], U32, name="v2_w", tag=tags[0], align_bytes=64)
-            plane = keep.tile([P, S2 // 2], U8, name="v2_s", tag=tags[1], align_bytes=64)
+        def pick_orbits(half, words_tag, plane_tag):
+            words = keep.tile([P, S2 // 2], U32, name="v2_w", tag=words_tag, align_bytes=64)
+            plane = keep.tile([P, S2 // 2], U8, name="v2_s", tag=plane_tag, align_bytes=64)
             picks = offs2_t[:, 32 * half : 32 * (half + 1)]
             nc.vector.tensor_copy(words[:], tab2_w[:].indirect(picks))
             nc.vector.tensor_copy(plane[:], tab2_planes[:].indirect(picks))
             v2_w.append(words)
             v2_s.append(plane)
 
-        pick_orbits(0, ("w4_raw01", "wgs_t"))
+        pick_orbits(0, raw_tag("w4", 0, 1), "wgs_t")
+
         page_q = []
         for half in range(2):
             pairs = turned[half][:].bitcast(F32).rearrange("n (b u p) -> n b u p", b=4, u=2)
             grouped = interleaved("mix%d" % half)
             grouped_pairs = grouped[:].bitcast(F32).rearrange("p (b n u) -> p b n u", b=4, u=2)
-            for two in range(2):
-                back = bank((6, 2, 0, 4)[2 * half + two], [P, 2, 2, P])
+            for b0, back_bank in ((0, 0), (2, 4)):
+                back = bank(back_bank, [P, 2, 2, P])
                 for b in range(2):
                     for u in range(2):
-                        nc.tensor.transpose(back[:, b, u, :], pairs[:, 2 * two + b, u, :], identity[:])
-                nc.scalar.copy(grouped_pairs[:, 2 * two : 2 * two + 2, :, :], back[:].rearrange("p b u n -> p b n u"))
-            page_q.append(quantise("page_q%d" % half, grouped, "page_q%d" % half))
+                        nc.tensor.transpose(back[:, b, u, :], pairs[:, b0 + b, u, :], identity[:])
+                nc.scalar.copy(grouped_pairs[:, b0 : b0 + 2, :, :], back[:].rearrange("p b u n -> p b n u"))
+            page_q.append(quantise("page_q%d" % half, grouped))
 
-        pick_orbits(1, ("wide", "mix1"))
+        pick_orbits(1, "wide", "mix1")
 
-        score_banks = ((1, 3), (3, 5), (5, 7), (7, 6), (1, 3), (5, 2), (0, 4), (7, 6))
-
-        def score_page(mb):
-            group, col = divmod(mb * P, S2 // 2)
-            scores = ring4.tile([P, T2], F32, name="scores")
+        def score_page(m):
+            half_list, col = divmod(m * P, S2 // 2)
+            scores = scores_pool.tile([P, T2], F32, name="scores")
             for half in range(2):
-                acc = bank(score_banks[mb][half], [P, BANK])
+                acc = bank(SCORE_BANKS[m][half], [P, BANK])
                 nc.tensor.matmul_mx(
                     out=acc[:],
-                    lhsT=v2_w[group][:, col : col + P].bitcast(FP8X4), lhsT_scale=v2_s[group][:, col : col + P],
+                    lhsT=v2_w[half_list][:, col : col + P].bitcast(FP8X4), lhsT_scale=v2_s[half_list][:, col : col + P],
                     rhs=page_q[half][0][:].bitcast(FP8X4), rhs_scale=page_q[half][1][:],
                     start=True, stop=True,
                 )
                 nc.scalar.copy(scores[:, half * BANK : (half + 1) * BANK], acc[:])
             return scores
 
-        def finish(mb, gap):
-            result = ring3.tile([P, PAIRS], F32, name="result")
-            nc.vector.scalar_tensor_tensor(result[:], gap[:], orbit_cols[:, mb : mb + 1], direct[mb], ALU.add, ALU.max)
-            nc.sync.dma_start(out[mb * P : (mb + 1) * P, :], result[:])
+        def lift_direct(m, f, direct):
+            nc.scalar.activation(direct, f[:], ACT.Identity, bias=orbit_cols[:, m : m + 1])
 
+        def finish(m, gap, direct):
+            result = result_pool.tile([P, PAIRS], F32, name="result")
+            nc.vector.scalar_tensor_tensor(result[:], gap[:], orbit_cols[:, m : m + 1], direct, ALU.add, ALU.max)
+            nc.sync.dma_start(out[m * P : (m + 1) * P, :], result[:])
+
+        second_tags = [raw_tag(name, chunk, a) for name in ("w2", "w1") for chunk in range(2) for a in range(PASSES)]
         gaps = []
         for chunk in range(S2 // CHUNK):
             pair = (2 * chunk, 2 * chunk + 1)
-            scores = [score_page(mb) for mb in pair]
+            scores = [score_page(m) for m in pair]
             seconds = []
-            for i, mb in enumerate(pair):
-                second = keep.tile([P, PAIRS], F32, name="second", tag=second_tags[mb], align_bytes=64)
+            for i, m in enumerate(pair):
+                second = keep.tile([P, PAIRS], F32, name="second", tag=second_tags[m], align_bytes=64)
                 nc.vector.tensor_copy(second[:], scores[i][:].indirect(pos2_t[:]))
                 seconds.append(second)
             if chunk > 0:
-                w4_q.append(quantise("w4_%d" % chunk, w4_mixed, "w4_%d" % chunk))
-                two = keep.tile([P, 2 * S], F32, name="two", tag="w4_raw%d1" % chunk, align_bytes=64)
-                for i, mb in enumerate(pair):
-                    score_directly(mb - 2, score_banks[pair[1]][i], two[:, i * S : (i + 1) * S])
-                for mb in pair:
-                    finish(mb - 2, gaps[mb - 2])
-            for i, mb in enumerate(pair):
-                gap = ring2.tile([P, PAIRS], F32, name="gap")
+                w4_q.append(quantise("w4_%d" % chunk, w4_mix))
+                directs = keep.tile([P, 2 * S], F32, name="directs", tag=raw_tag("w4", chunk, 1), align_bytes=64)
+                if chunk > 1:
+                    f_pair = [fp8_product(w4_q, m - 2, SCORE_BANKS[pair[1]][i]) for i, m in enumerate(pair)]
+                for i, m in enumerate(pair):
+                    lift_direct(m - 2, f_pair[i], directs[:, i * S : (i + 1) * S])
+                for i, m in enumerate(pair):
+                    finish(m - 2, gaps[m - 2], directs[:, i * S : (i + 1) * S])
+            for i, m in enumerate(pair):
+                gap = gap_pool.tile([P, PAIRS], F32, name="gap")
                 nc.vector.tensor_tensor(gap[:], scores[i][:].indirect(pos1_t[:]), seconds[i][:], ALU.subtract)
                 gaps.append(gap)
             if chunk + 1 < S2 // CHUNK:
-                w4_mixed = interleaved(second_tags[pair[0]])
-                cast_weight(w4_raw[chunk + 1], w4_mixed)
-        two = keep.tile([P, 2 * S], F32, name="two", tag="w4_raw00", align_bytes=64)
-        for i, mb in enumerate(pair):
-            score_directly(mb, score_banks[0][i], two[:, i * S : (i + 1) * S])
-        for mb in pair:
-            finish(mb, gaps[mb])
+                w4_mix = interleaved(second_tags[pair[0]])
+                round_weight(w4_raw[chunk + 1], w4_mix)
+        directs = keep.tile([P, 2 * S], F32, name="directs", tag=raw_tag("w4", 0, 0), align_bytes=64)
+        for i, m in enumerate(pair):
+            lift_direct(m, fp8_product(w4_q, m, SCORE_BANKS[0][i]), directs[:, i * S : (i + 1) * S])
+        for i, m in enumerate(pair):
+            finish(m, gaps[m], directs[:, i * S : (i + 1) * S])

import math
from contextlib import ExitStack

import concourse.mybir as mybir
from concourse.masks import make_identity

K, T, S, H, T2, S2, T3, PAIRS = 1024, 2048, 512, 512, 1024, 1024, 2048, 512
FLOPS = 2 * (3 * K * H * S + H * S2 * T2 + K * S2 * S)

F32 = mybir.dt.float32
BF16 = mybir.dt.bfloat16
I32 = mybir.dt.int32
U32 = mybir.dt.uint32
U16 = mybir.dt.uint16
U8 = mybir.dt.uint8
FP8X4 = mybir.dt.float8_e4m3fn_x4
FP4X4 = mybir.dt.float4_e2m1fn_x4
ALU = mybir.AluOpType
ACT = mybir.ActivationFunctionType

P = 128
PACK = 4
K_PASS = P * PACK
PASSES = K // K_PASS
BANK = 512
CHUNK = 256
QUADS = 4
TURN = 2.0 * math.pi
LIFT = 1.5 * 2.0**23

SCORE_BANKS = ((1, 3), (3, 2), (2, 7), (7, 0), (1, 3), (4, 5), (0, 2), (7, 6))


def tile_list_tracklet_orbit_features_kernel(
    tc, tab_words, tab_scales, offs, tab2_words, tab2_scales, offs2, offs3, pos1, pos2,
    w1, w2, w3_words, w3_scales, w4, wgs, page0, orbit, out,
):
    nc = tc.nc
    with ExitStack() as ctx:
        keep = ctx.enter_context(tc.tile_pool(name="keep", bufs=1))
        scores_pool = ctx.enter_context(tc.tile_pool(name="scores_pool", bufs=4))
        result_pool = ctx.enter_context(tc.tile_pool(name="result_pool", bufs=3))
        gap_pool = ctx.enter_context(tc.tile_pool(name="gap_pool", bufs=2))
        psum = ctx.enter_context(tc.psum_pool(name="psum", bufs=1))

        def bank(b, shape):
            return psum.tile(shape, F32, name="bank%d" % b, tag="bank%d" % b)

        def raw_tag(name, chunk, a):
            return "%s_raw%d%d" % (name, chunk, a)

        def interleaved(tag, words=BANK):
            return keep.tile([P, words * PACK], BF16, name=tag, tag=tag, align_bytes=64)

        def work(name, q, dtype, tag=None):
            return keep.tile([P, S], dtype, name=name, tag=tag or "%s%d" % (name, q % 2), align_bytes=64)

        def load_list(name, src):
            tile = keep.tile(list(src.shape), U16, name=name)
            nc.sync.dma_start(tile[:], src)
            return tile

        def cleared_planes(name, src, engine):
            planes = keep.tile([P, src.shape[0] * src.shape[2]], U8, name=name, align_bytes=64)
            engine.memset(planes[:].bitcast(I32), 0)
            return planes

        def load_scale_rows(planes, src):
            for quad in range(QUADS):
                nc.sync.dma_start(
                    planes[32 * quad : 32 * quad + 4, :].bitcast(I32).rearrange("r (a c) -> r a c", a=src.shape[0]),
                    src[:, 4 * quad : 4 * quad + 4, :].bitcast(I32).rearrange("a r c -> r a c"),
                )

        def load_words(name, src):
            tile = keep.tile([P, src.shape[1]], U32, name=name, align_bytes=64)
            nc.sync.dma_start(tile[:].bitcast(I32), src.rearrange("p t i -> p (t i)").bitcast(I32))
            return tile

        def load_chunk(name, w, chunk):
            tiles = []
            for a in range(PASSES):
                raw = keep.tile([P, PACK, CHUNK], F32, name="raw", tag=raw_tag(name, chunk, a), align_bytes=64)
                rows = w[a * K_PASS : (a + 1) * K_PASS, chunk * CHUNK : (chunk + 1) * CHUNK]
                nc.sync.dma_start(raw[:], rows.rearrange("(p t) c -> p t c", t=PACK))
                tiles.append(raw)
            return tiles

        def load_page(q):
            tile = keep.tile([P, T2], F32, name="page%d" % q)
            nc.sync.dma_start(tile[:], page0[q * P : (q + 1) * P, :])
            return tile

        tab_planes = cleared_planes("tab_planes", tab_scales, nc.vector)
        warm = keep.tile([P, 2], F32, name="warm")
        nc.vector.memset(warm[:, 0:1], 0.0)
        nc.scalar.activation(warm[:, 1:2], warm[:, 0:1], ACT.Silu)
        w3_planes = cleared_planes("w3_planes", w3_scales, nc.gpsimd)
        tab2_planes = cleared_planes("tab2_planes", tab2_scales, nc.gpsimd)
        identity = keep.tile([P, P], F32, name="identity")
        make_identity(nc, identity[:])

        tab_w = [load_words("tab_w0", tab_words[0])]
        offs_t = load_list("offs_t", offs)
        load_scale_rows(tab_planes, tab_scales)
        w2_raw = [load_chunk("w2", w2, 0)]
        tab_w.append(load_words("tab_w1", tab_words[1]))
        load_scale_rows(w3_planes, w3_scales)
        w1_raw = [load_chunk("w1", w1, 0)]
        w3_w = keep.tile([P, PASSES * 2 * H], U8, name="w3_w", align_bytes=64)
        nc.sync.dma_start(
            w3_w[:].bitcast(I32).rearrange("p (a c) -> p a c", a=PASSES),
            w3_words.bitcast(I32).rearrange("a p c -> p a c"),
        )
        wgs_t = keep.tile([P, S], F32, name="wgs_t", tag="wgs_t", align_bytes=64)
        nc.sync.dma_start(wgs_t[:], wgs)
        offs3_t = load_list("offs3_t", offs3)
        page = [load_page(0)]
        w2_raw.append(load_chunk("w2", w2, 1))
        w1_raw.append(load_chunk("w1", w1, 1))
        page.append(load_page(1))
        page.append(load_page(2))
        w4_raw = [load_chunk("w4", w4, 0)]
        page.append(load_page(3))
        offs2_t = load_list("offs2_t", offs2)
        tab2_w = load_words("tab2_w", tab2_words[0])
        load_scale_rows(tab2_planes, tab2_scales)
        pos1_t = load_list("pos1_t", pos1)
        pos2_t = load_list("pos2_t", pos2)
        orbit_cols = keep.tile([P, S2 // P], F32, name="orbit_cols")
        with nc.allow_non_contiguous_dma(reason="one value of orbit to a partition and row block"):
            nc.sync.dma_start(orbit_cols[:], orbit.rearrange("(c p) -> p c", p=P))
        for chunk in range(1, S2 // CHUNK):
            w4_raw.append(load_chunk("w4", w4, chunk))

        def round_weight(raw_passes, grouped):
            for a in range(PASSES):
                dst = grouped[:, a * CHUNK * PACK : (a + 1) * CHUNK * PACK]
                nc.scalar.copy(
                    dst.rearrange("p (c i t) -> p c t i", i=4, t=PACK),
                    raw_passes[a][:].rearrange("p t (c i) -> p c t i", i=4),
                )

        def quantise(name, grouped, pieces=1):
            words = grouped.shape[1] // PACK
            codes = keep.tile([P, words], U32, name=name + "_codes", align_bytes=64)
            scales = keep.tile([P, words], U8, name=name + "_scales", align_bytes=64)
            step = words // pieces
            for w0 in range(0, words, step):
                nc.vector.quantize_mx(
                    out=codes[:, w0 : w0 + step].bitcast(FP8X4), scales=scales[:, w0 : w0 + step],
                    in_=grouped[:, PACK * w0 : PACK * (w0 + step)],
                )
            return codes, scales

        v_w, v_s = [], []
        for a in range(PASSES):
            words = keep.tile([P, S], U32, name="v_w%d" % a, align_bytes=64)
            plane = keep.tile([P, S], U8, name="v_s%d" % a, align_bytes=64)
            nc.vector.tensor_copy(words[:], tab_w[a][:].indirect(offs_t[:]))
            nc.vector.tensor_copy(plane[:], tab_planes[:, a * T : (a + 1) * T].indirect(offs_t[:]))
            v_w.append(words)
            v_s.append(plane)

        def fp8_product(chunks, block, b):
            chunk, col = divmod(block * P, CHUNK)
            codes, scales = chunks[chunk]
            acc = bank(b, [P, S])
            for a in range(PASSES):
                cols = slice(a * CHUNK + col, a * CHUNK + col + P)
                nc.tensor.matmul_mx(
                    out=acc[:], lhsT=codes[:, cols].bitcast(FP8X4), lhsT_scale=scales[:, cols],
                    rhs=v_w[a][:].bitcast(FP8X4), rhs_scale=v_s[a][:],
                    start=(a == 0), stop=(a == PASSES - 1),
                )
            return acc

        def fp4_product(q, b):
            acc = bank(b, [P, S])
            for a in range(PASSES):
                nc.tensor.matmul_mx(
                    out=acc[:],
                    lhsT=w3_w[:, 2 * (a * H + q * P) : 2 * (a * H + (q + 1) * P)].bitcast(FP4X4),
                    lhsT_scale=w3_planes[:, a * H + q * P : a * H + (q + 1) * P],
                    rhs=v_w[a][:].bitcast(FP8X4), rhs_scale=v_s[a][:],
                    start=(a == 0), stop=(a == PASSES - 1),
                )
            return acc

        def turns_on_vector(q, p2):
            whole = work("whole", q, I32)
            nc.vector.tensor_scalar(whole[:], p2[:], 1.0 / TURN, None, ALU.mult)
            return whole

        def turns_on_scalar(q, p2):
            lifted = work("lifted", q, U32)
            nc.scalar.activation(lifted[:], p2[:], ACT.Copy, scale=1.0 / TURN, bias=LIFT)
            whole = work("whole", q, F32)
            nc.scalar.activation(whole[:], lifted[:], ACT.Copy, bias=-LIFT)
            return whole

        def part_turn(q, p2, whole, tag=None):
            part = work("part", q, F32, tag)
            nc.vector.scalar_tensor_tensor(part[:], p2[:], 1.0 / TURN, whole[:], ALU.mult, ALU.subtract)
            return part

        def difference(q, p1, part, sine_tag=None, tanh_tag=None):
            sine = work("sine", q, F32, sine_tag)
            nc.scalar.activation(sine[:], part[:], ACT.Sin, scale=TURN)
            tanh = work("tanh", q, F32, tanh_tag)
            nc.scalar.activation(tanh[:], p1[:], ACT.Tanh)
            diff = work("diff", q, F32)
            nc.vector.tensor_tensor(diff[:], tanh[:], sine[:], ALU.subtract)
            return diff

        def renew(q, diff, p3, h_tag=None):
            h = work("h", q, F32, h_tag)
            nc.vector.tensor_tensor(h[:], p3[:], diff[:], ALU.mult)
            nc.vector.tensor_tensor(page[q][:].indirect(offs3_t[:]), h[:], wgs_t[:], ALU.mult)

        mix = [interleaved("mix0")]
        round_weight(w2_raw[0], mix[0])
        w2_q = [quantise("w2_0", mix[0])]
        mix.append(interleaved("mix1"))
        round_weight(w1_raw[0], mix[1])
        w1_q = [quantise("w1_0", mix[1], pieces=PASSES)]
        p2 = [fp8_product(w2_q, 0, 0), fp8_product(w2_q, 1, 1)]
        p1 = [fp8_product(w1_q, 0, 2), fp8_product(w1_q, 1, 3)]
        part = part_turn(0, p2[0], turns_on_vector(0, p2[0]))
        diff = difference(0, p1[0], part, sine_tag=raw_tag("w1", 0, 1), tanh_tag="wide")
        part = part_turn(1, p2[1], turns_on_vector(1, p2[1]), tag="mix1")
        renew(0, diff, fp4_product(0, 1))
        diff = difference(1, p1[1], part)
        p3 = fp4_product(1, 2)

        wide = interleaved("wide", 2 * BANK)
        round_weight(w2_raw[1], wide[:, : BANK * PACK])
        round_weight(w1_raw[1], wide[:, BANK * PACK :])
        codes, scales = quantise("w21_1", wide)
        w2_q.append((codes[:, :BANK], scales[:, :BANK]))
        w1_q.append((codes[:, BANK:], scales[:, BANK:]))
        renew(1, diff, p3, h_tag="wide")

        p2 = [fp8_product(w2_q, 2, 7), fp8_product(w2_q, 3, 0)]
        p1 = [fp8_product(w1_q, 2, 6), fp8_product(w1_q, 3, 5)]
        p3 = [fp4_product(2, 3), fp4_product(3, 2)]
        wholes = [turns_on_scalar(2 + i, p2[i]) for i in range(2)]
        diffs = []
        for i, part_tag in enumerate(("lifted1", "wide")):
            diffs.append(difference(2 + i, p1[i], part_turn(2 + i, p2[i], wholes[i], part_tag)))
        renew(2, diffs[0], p3[0])
        w4_mix = interleaved("sine0")
        round_weight(w4_raw[0], w4_mix)
        renew(3, diffs[1], p3[1], h_tag=raw_tag("w4", 0, 1))
        w4_q = [quantise("w4_0", w4_mix)]

        turned = [interleaved("wide"), interleaved("turned1")]

        def turn(q, banks):
            for half in range(2):
                flip = bank(banks[half], [P, 4, P])
                for b in range(4):
                    n0 = half * BANK + b * P
                    nc.tensor.transpose(flip[:, b, :], page[q][:, n0 : n0 + P], identity[:])
                dst = turned[half][:].rearrange("n (b u p e) -> n b u p e", b=4, u=2, e=2)
                nc.scalar.copy(
                    dst[:, :, :, 32 * q : 32 * (q + 1), :],
                    flip[:].rearrange("n b (p u e) -> n b u p e", u=2, e=2),
                )

        turn(0, (7, 7))
        turn(1, (0, 7))
        turn(2, (0, 4))
        f_pair = [fp8_product(w4_q, 0, 6), fp8_product(w4_q, 1, 5)]
        turn(3, (2, 7))

        v2_w, v2_s = [], []

        def pick_orbits(half, words_tag, plane_tag):
            words = keep.tile([P, S2 // 2], U32, name="v2_w", tag=words_tag, align_bytes=64)
            plane = keep.tile([P, S2 // 2], U8, name="v2_s", tag=plane_tag, align_bytes=64)
            picks = offs2_t[:, 32 * half : 32 * (half + 1)]
            nc.vector.tensor_copy(words[:], tab2_w[:].indirect(picks))
            nc.vector.tensor_copy(plane[:], tab2_planes[:].indirect(picks))
            v2_w.append(words)
            v2_s.append(plane)

        pick_orbits(0, raw_tag("w4", 0, 1), "wgs_t")

        page_q = []
        for half in range(2):
            pairs = turned[half][:].bitcast(F32).rearrange("n (b u p) -> n b u p", b=4, u=2)
            grouped = interleaved("mix%d" % half)
            grouped_pairs = grouped[:].bitcast(F32).rearrange("p (b n u) -> p b n u", b=4, u=2)
            for b0, back_bank in ((0, 0), (2, 4)):
                back = bank(back_bank, [P, 2, 2, P])
                for b in range(2):
                    for u in range(2):
                        nc.tensor.transpose(back[:, b, u, :], pairs[:, b0 + b, u, :], identity[:])
                nc.scalar.copy(grouped_pairs[:, b0 : b0 + 2, :, :], back[:].rearrange("p b u n -> p b n u"))
            page_q.append(quantise("page_q%d" % half, grouped))

        pick_orbits(1, "wide", "mix1")

        def score_page(m):
            half_list, col = divmod(m * P, S2 // 2)
            scores = scores_pool.tile([P, T2], F32, name="scores")
            for half in range(2):
                acc = bank(SCORE_BANKS[m][half], [P, BANK])
                nc.tensor.matmul_mx(
                    out=acc[:],
                    lhsT=v2_w[half_list][:, col : col + P].bitcast(FP8X4), lhsT_scale=v2_s[half_list][:, col : col + P],
                    rhs=page_q[half][0][:].bitcast(FP8X4), rhs_scale=page_q[half][1][:],
                    start=True, stop=True,
                )
                nc.scalar.copy(scores[:, half * BANK : (half + 1) * BANK], acc[:])
            return scores

        def lift_direct(m, f, direct):
            nc.scalar.activation(direct, f[:], ACT.Identity, bias=orbit_cols[:, m : m + 1])

        def finish(m, gap, direct):
            result = result_pool.tile([P, PAIRS], F32, name="result")
            nc.vector.scalar_tensor_tensor(result[:], gap[:], orbit_cols[:, m : m + 1], direct, ALU.add, ALU.max)
            nc.sync.dma_start(out[m * P : (m + 1) * P, :], result[:])

        second_tags = [raw_tag(name, chunk, a) for name in ("w2", "w1") for chunk in range(2) for a in range(PASSES)]
        gaps = []
        for chunk in range(S2 // CHUNK):
            pair = (2 * chunk, 2 * chunk + 1)
            scores = [score_page(m) for m in pair]
            seconds = []
            for i, m in enumerate(pair):
                second = keep.tile([P, PAIRS], F32, name="second", tag=second_tags[m], align_bytes=64)
                nc.vector.tensor_copy(second[:], scores[i][:].indirect(pos2_t[:]))
                seconds.append(second)
            if chunk > 0:
                w4_q.append(quantise("w4_%d" % chunk, w4_mix))
                directs = keep.tile([P, 2 * S], F32, name="directs", tag=raw_tag("w4", chunk, 1), align_bytes=64)
                if chunk > 1:
                    f_pair = [fp8_product(w4_q, m - 2, SCORE_BANKS[pair[1]][i]) for i, m in enumerate(pair)]
                for i, m in enumerate(pair):
                    lift_direct(m - 2, f_pair[i], directs[:, i * S : (i + 1) * S])
                for i, m in enumerate(pair):
                    finish(m - 2, gaps[m - 2], directs[:, i * S : (i + 1) * S])
            for i, m in enumerate(pair):
                gap = gap_pool.tile([P, PAIRS], F32, name="gap")
                nc.vector.tensor_tensor(gap[:], scores[i][:].indirect(pos1_t[:]), seconds[i][:], ALU.subtract)
                gaps.append(gap)
            if chunk + 1 < S2 // CHUNK:
                w4_mix = interleaved(second_tags[pair[0]])
                round_weight(w4_raw[chunk + 1], w4_mix)
        directs = keep.tile([P, 2 * S], F32, name="directs", tag=raw_tag("w4", 0, 0), align_bytes=64)
        for i, m in enumerate(pair):
            lift_direct(m, fp8_product(w4_q, m, SCORE_BANKS[0][i]), directs[:, i * S : (i + 1) * S])
        for i, m in enumerate(pair):
            finish(m, gaps[m], directs[:, i * S : (i + 1) * S])
